import numpy as np
import ml_dtypes


def mxq(x, axis, fmt="e4m3"):
    dtype, down = {"e4m3": (ml_dtypes.float8_e4m3fn, 7), "e5m2": (ml_dtypes.float8_e5m2, 14)}[fmt]
    v = np.moveaxis(np.asarray(x, np.float32).astype(ml_dtypes.bfloat16).astype(np.float64), axis, -1)
    blocks = v.reshape(v.shape[:-1] + (-1, 32))
    amax = np.abs(blocks).max(-1, keepdims=True)
    byte = np.maximum(np.where(amax > 0, np.frexp(amax)[1] - 1 + 127, 0) - down, 1)
    scale = np.exp2(byte - 127.0)
    codes = (blocks / scale).astype(np.float32).astype(dtype).astype(np.float64)
    return np.moveaxis((codes * scale).reshape(v.shape), -1, axis)


WIDE = False


def mx_kscale(k):
    if not WIDE:
        return np.ones(k)
    levels = np.array([10, -10, 5, -5, 0])
    if k % 512:
        return np.exp2(np.random.permutation(np.resize(levels, k // 32))).repeat(32)
    a = np.empty((k // 512, 16))
    for p in range(k // 512):
        a[p, :8] = np.random.permutation(np.resize(levels, 8))
        for g in range(8):
            far = levels[np.abs(levels - a[p, g]) >= 10]
            a[p, g + 8] = far[np.random.randint(len(far))]
    return np.exp2(a.ravel()).repeat(32)


def f64(x):
    return np.asarray(x).astype(np.float64)


def striped(idx):
    return np.tile(idx.reshape(-1, 16).T, (8, 1)).astype(np.uint16)


def unstriped(offs):
    return offs[:16].T.reshape(-1).astype(np.int64)


E2M1 = np.array([0.0, 0.5, 1.0, 1.5, 2.0, 3.0, 4.0, 6.0, -0.0, -0.5, -1.0, -1.5, -2.0, -3.0, -4.0, -6.0])


def pack_weight(w, fmt):
    k, n = w.shape
    w = f64(np.asarray(w, np.float32).astype(ml_dtypes.bfloat16)).reshape(k // 32, 32, n)
    amax = np.abs(w).max(1)
    if fmt == "e4m3":
        byte = np.frexp(amax)[1] - 1 + 127 - 7
    else:
        mant, ex = np.frexp(amax / 6.0)
        byte = np.where(mant > 0.5, ex, ex - 1) + 127
    byte = np.clip(np.where(amax > 0, byte, 1), 1, 254)
    scaled = (w * np.exp2(127.0 - byte)[:, None, :]).reshape(k, n).astype(np.float32)
    by_word = np.ascontiguousarray(scaled.reshape(k // 512, 128, 4, n).transpose(0, 1, 3, 2))
    if fmt == "e4m3":
        words = by_word.astype(ml_dtypes.float8_e4m3fn).view(np.uint8)
    else:
        c = by_word.astype(ml_dtypes.float4_e2m1fn).view(np.uint8) & 0xF
        words = (c[..., 0::2] | (c[..., 1::2] << 4)).reshape(k // 512, 128, 2 * n)
    return np.ascontiguousarray(words), np.ascontiguousarray(byte.astype(np.uint8).reshape(k // 512, 16, n))


def unpack_weight(words, scales, fmt):
    g, _, n = scales.shape
    words = np.ascontiguousarray(words).reshape(g, 128, n, -1)
    if fmt == "e4m3":
        vals = words.view(ml_dtypes.float8_e4m3fn).astype(np.float64)
    else:
        nib = np.empty((g, 128, n, 4), np.uint8)
        nib[..., 0::2] = words & 0xF
        nib[..., 1::2] = words >> 4
        vals = E2M1[nib]
    vals = vals * np.repeat(np.exp2(scales.astype(np.float64) - 127.0), 8, axis=1)[..., None]
    return vals.transpose(0, 1, 3, 2).reshape(g * 512, n)


def gelu(v):
    return 0.5 * v * (1.0 + np.tanh(np.sqrt(2.0 / np.pi) * (v + 0.044715 * v**3)))


K, H, N, T, S, P, T2 = 1024, 1536, 768, 2048, 512, 512, 1024

def setup_inputs():
    n = np.random.standard_normal
    s = mx_kscale(K)[:, None]
    u = mx_kscale(H)[:, None]
    d = {}
    d["tab_words"], d["tab_scales"] = pack_weight(n((K, T)) * s, "e4m3")
    d["w1_words"], d["w1_scales"] = pack_weight(n((K, H)) / s / K**0.5, "e2m1")
    d["gain"] = (0.7 * n(H)).astype(np.float32)
    d["wgs"] = np.exp(0.3 * n((128, S))).astype(np.float32)
    d["page0"] = (1.2 * n((H, T2))).astype(np.float32)
    d["shift"] = (0.8 * n(H)).astype(np.float32)
    d["risk"] = (np.exp(0.3 * n(H)) * u[:, 0]).astype(np.float32)
    d["w2"] = (1.2 * n((H, N)) / u / H**0.5).astype(np.float32)
    d["wgo"] = np.exp(0.3 * n((128, P))).astype(np.float32)
    d["page1"] = n((N, T2)).astype(np.float32)
    d["offs"] = striped(np.random.permutation(T)[:S])
    d["offs2"] = striped(np.random.permutation(T2)[:S])
    d["offs3"] = striped(np.random.permutation(T2)[:P])
    d["offs4"] = striped(np.random.permutation(T2)[:P])
    return d

def reference(tab_words, tab_scales, w1_words, w1_scales, gain, wgs, page0, shift, risk, w2, wgo, page1, offs, offs2, offs3, offs4):
    v = unpack_weight(tab_words, tab_scales, "e4m3")[:, unstriped(offs)]
    w1 = unpack_weight(w1_words, w1_scales, "e2m1")
    f = w1.T @ v
    h = f64(gain)[:, None] * np.square(f)
    page = f64(page0).copy()
    page[:, unstriped(offs2)] = np.tile(f64(wgs), (H // 128, 1)) * h
    x = page[:, unstriped(offs3)]
    z = f64(risk)[:, None] * np.tanh(x + f64(shift)[:, None])
    y = mxq(f64(w2), 0, "e4m3").T @ mxq(z, 0, "e4m3")
    out = f64(page1).copy()
    out[:, unstriped(offs4)] = np.tile(f64(wgo), (N // 128, 1)) * y
    return out

@@ -1,0 +1,268 @@
+from contextlib import ExitStack
+
+import concourse.mybir as mybir
+from concourse.masks import make_identity
+
+K, H, N, T, S, M, T2 = 1024, 1536, 768, 2048, 512, 512, 1024
+FLOPS = 2 * K * H * S + 2 * H * N * M
+
+F32 = mybir.dt.float32
+BF16 = mybir.dt.bfloat16
+I32 = mybir.dt.int32
+U32 = mybir.dt.uint32
+U16 = mybir.dt.uint16
+U8 = mybir.dt.uint8
+FP8X4 = mybir.dt.float8_e4m3fn_x4
+FP4X4 = mybir.dt.float4_e2m1fn_x4
+ACT = mybir.ActivationFunctionType
+MULT = mybir.AluOpType.mult
+
+P = 128
+PACK = 4
+PASS = P * PACK
+K_PASSES = K // PASS
+R_PASSES = H // PASS
+SLICES = R_PASSES * PACK
+J_TILES = S // P
+N_TILES = N // P
+N_BLOCK = 256
+N_BLOCKS = N // N_BLOCK
+QUADS = 4
+HALF = S // 2
+ALIGN = 64
+
+
+def tile_list_abort_page_scores_kernel(
+    tc, tab_words, tab_scales, w1_words, w1_scales, gain, wgs, page0, shift, risk, w2, wgo, page1,
+    offs, offs2, offs3, offs4, out,
+):
+    nc = tc.nc
+    with ExitStack() as ctx:
+        keep = ctx.enter_context(tc.tile_pool(name="keep", bufs=1))
+        ring = ctx.enter_context(tc.tile_pool(name="ring", bufs=2))
+        psum = ctx.enter_context(tc.psum_pool(name="psum", bufs=2))
+
+        def load_list(src, name):
+            lst = keep.tile([P, S // 16], U16, name=name)
+            nc.sync.dma_start(lst[:], src)
+            return lst
+
+        def load_per_row(queue, vec, name):
+            col = keep.tile([P, R_PASSES, PACK], F32, name=name)
+            queue.dma_start(col[:], vec.rearrange("(b p t) -> p b t", p=P, t=PACK))
+            return col
+
+        def load_scale_rows(queue, plane, scales):
+            for q in range(QUADS):
+                queue.dma_start(
+                    plane[32 * q : 32 * q + 4, :, :].bitcast(I32),
+                    scales[:, 4 * q : 4 * q + 4, :].rearrange("a r c -> r a c").bitcast(I32),
+                )
+
+        page0_rows = page0.rearrange("(b p t) c -> b t p c", p=P, t=PACK)
+
+        def load_page0(i):
+            page = keep.tile([P, T2], F32, name=f"page0_{i}")
+            nc.sync.dma_start(page[:], page0_rows[i // PACK, i % PACK])
+            return page
+
+        def load_w1(b):
+            words = keep.tile([P, K_PASSES, 2 * PASS], U8, name=f"w1_words_{b}", align_bytes=ALIGN)
+            nc.sync.dma_start(
+                words[:].bitcast(I32),
+                w1_words[:, :, 2 * PASS * b : 2 * PASS * (b + 1)].rearrange("a p c -> p a c").bitcast(I32),
+            )
+            return words
+
+        tab_plane = keep.tile([P, K_PASSES, T], U8, name="tab_plane", align_bytes=ALIGN)
+        nc.vector.memset(tab_plane[:].bitcast(I32), 0)
+        w1_plane_first = keep.tile([P, K_PASSES, PASS], U8, name="w1_plane_first", align_bytes=ALIGN)
+        nc.vector.memset(w1_plane_first[:].bitcast(I32), 0)
+        w1_plane_rest = keep.tile([P, K_PASSES, H - PASS], U8, name="w1_plane_rest", align_bytes=ALIGN)
+        nc.gpsimd.memset(w1_plane_rest[:].bitcast(I32), 0)
+        w1_planes = [w1_plane_first] + [w1_plane_rest[:, :, PASS * b : PASS * (b + 1)] for b in range(R_PASSES - 1)]
+        ident = keep.tile([P, P], F32, name="ident")
+        make_identity(nc, ident[:])
+
+        def load_tab(a):
+            words = keep.tile([P, T], I32, name=f"tab_{a}")
+            nc.sync.dma_start(words[:], tab_words[a].rearrange("p t i -> p (t i)").bitcast(I32))
+            return words
+
+        wgs_rows = wgs.rearrange("(m t) j -> m t j", t=PACK)
+        wgs_first = keep.tile([P, 1, S], F32, name="wgs_first")
+        wgs_rest = keep.tile([P, PACK - 1, S], F32, name="wgs_rest")
+
+        def load_wgs(dealt, rows, quads):
+            for q in quads:
+                nc.sync.dma_start(dealt[32 * q : 32 * (q + 1)], rows)
+
+        idx = load_list(offs, "idx")
+        tab = [load_tab(0)]
+        load_scale_rows(nc.sync, tab_plane, tab_scales)
+        w1 = [load_w1(0)]
+        load_scale_rows(nc.sync, w1_plane_first, w1_scales[:, :, 0:PASS])
+        tab.append(load_tab(1))
+        gain_col = load_per_row(nc.sync, gain, "gain_col")
+        idx2 = load_list(offs2, "idx2")
+        pages = [load_page0(0)]
+        load_wgs(wgs_first, wgs_rows[:, 0:1, :], range(QUADS))
+        idx3 = load_list(offs3, "idx3")
+        pages.append(load_page0(1))
+        load_wgs(wgs_rest, wgs_rows[:, 1:PACK, :], range(QUADS))
+        wgs_dealt = [wgs_first[:, 0, :]] + [wgs_rest[:, t, :] for t in range(PACK - 1)]
+        shift_col = load_per_row(nc.sync, shift, "shift_col")
+        risk_col = load_per_row(nc.sync, risk, "risk_col")
+        load_scale_rows(nc.sync, w1_plane_rest, w1_scales[:, :, PASS:H])
+        w1 += [load_w1(b) for b in range(1, R_PASSES)]
+
+        v_scales, v_words = {}, {}
+        for half in range(2):
+            entries = idx[:, HALF // 16 * half : HALF // 16 * (half + 1)]
+            for a in range(K_PASSES):
+                picked = keep.tile([P, HALF], U8, name=f"v_scales_{a}_{half}", align_bytes=ALIGN)
+                nc.vector.tensor_copy(picked[:], tab_plane[:, a, :].indirect(entries))
+                v_scales[a, half] = picked
+            for a in range(K_PASSES):
+                picked = keep.tile([P, HALF], U32, name=f"v_words_{a}_{half}", align_bytes=ALIGN)
+                nc.vector.tensor_copy(picked[:], tab[a][:].bitcast(U32).indirect(entries))
+                v_words[a, half] = picked
+
+        def product(b, jt):
+            half, cols = jt // 2, slice(P * (jt % 2), P * (jt % 2 + 1))
+            f = psum.tile([P, PASS], F32, name="f", bufs=4)
+            for a in range(K_PASSES):
+                nc.tensor.matmul_mx(
+                    out=f[:],
+                    lhsT=v_words[a, half][:, cols].bitcast(FP8X4),
+                    lhsT_scale=v_scales[a, half][:, cols],
+                    rhs=w1[b][:, a, :].bitcast(FP4X4),
+                    rhs_scale=w1_planes[b][:, a, :],
+                    start=(a == 0),
+                    stop=(a == K_PASSES - 1),
+                )
+            return f[:].rearrange("j (p t) -> j t p", t=PACK)
+
+        def square(f, name, t0, t1):
+            sq = ring.tile([P, t1 - t0, P], F32, name=name)
+            nc.scalar.activation(sq[:], f[:, t0:t1, :], ACT.Square)
+            return [sq[:, t, :] for t in range(t1 - t0)]
+
+        def turn(h_cols, parts, b, t):
+            turned = psum.tile([P, P * len(parts)], F32, name="turned")
+            for u, part in enumerate(parts):
+                nc.tensor.transpose(turned[:, P * u : P * (u + 1)], part, ident[:])
+            nc.scalar.activation(h_cols, turned[:], ACT.Copy, scale=gain_col[:, b, t : t + 1])
+
+        h = [keep.tile([P, S], F32, name=f"h_{i}", tag=f"slot_{i}", align_bytes=ALIGN) for i in range(SLICES)]
+        f0 = []
+        for half in range(2):
+            f0 += [product(0, jt) for jt in (2 * half, 2 * half + 1)]
+            parts = [square(f0[jt], f"single_{jt}", 0, 1)[0] for jt in (2 * half, 2 * half + 1)]
+            turn(h[0][:, HALF * half : HALF * (half + 1)], parts, 0, 0)
+        for t in range(1, PACK):
+            turn(h[t][:], [square(f0[jt], f"single_{jt}", t, t + 1)[0] for jt in range(J_TILES)], 0, t)
+        for b in range(1, R_PASSES):
+            squares = [square(product(b, jt), f"square_{jt}", 0, PACK) for jt in range(J_TILES)]
+            for t in range(PACK):
+                turn(h[PACK * b + t][:], [squares[jt][t] for jt in range(J_TILES)], b, t)
+
+        w2_bf = keep.tile([P, N_BLOCKS, R_PASSES, N_BLOCK * PACK], BF16, name="w2_bf", align_bytes=ALIGN)
+        w2_rows = w2.rearrange("(b p t) n -> b p t n", p=P, t=PACK)
+
+        def round_w2(piece):
+            nb, b = divmod(piece, R_PASSES)
+            raw = ring.tile([P, PACK, N_BLOCK], F32, name="w2_raw", bufs=3)
+            nc.sync.dma_start(raw[:], w2_rows[b, :, :, N_BLOCK * nb : N_BLOCK * (nb + 1)])
+            nc.scalar.copy(
+                w2_bf[:, nb, b, :].rearrange("p (c i t) -> p c t i", i=4, t=PACK),
+                raw[:].rearrange("p t (c i) -> p c t i", i=4),
+            )
+
+        z_bf = []
+
+        def recall(i):
+            b, t = divmod(i, PACK)
+            tag = f"slot_{i + 1}" if i < SLICES - 2 else f"x_{i}"
+            x = keep.tile([P, M], F32, name=f"x_{i}", tag=tag, align_bytes=ALIGN)
+            nc.vector.tensor_copy(x[:], pages[i][:].indirect(idx3[:]))
+            bent = ring.tile([P, M], F32, name="bent")
+            nc.scalar.activation(bent[:], x[:], ACT.Tanh, bias=shift_col[:, b, t : t + 1])
+            if t == 0:
+                z_bf.append(keep.tile([P, M, PACK], BF16, name=f"z_bf_{b}", align_bytes=ALIGN))
+            nc.scalar.activation(z_bf[b][:, :, t], bent[:], ACT.Copy, scale=risk_col[:, b, t : t + 1])
+
+        for i in range(SLICES):
+            if i >= 2:
+                pages.append(load_page0(i))
+                if i - 2 < N_BLOCKS * R_PASSES:
+                    round_w2(i - 2)
+            width = HALF if i == 0 else S
+            for j0 in range(0, S, width):
+                nc.vector.tensor_tensor(
+                    pages[i][:].indirect(idx2[:, j0 // 16 : (j0 + width) // 16]),
+                    h[i][:, j0 : j0 + width],
+                    wgs_dealt[i % PACK][:, j0 : j0 + width],
+                    MULT,
+                )
+            if i >= 1:
+                recall(i - 1)
+        recall(SLICES - 1)
+
+        wgo_sb = keep.tile([P, M], F32, name="wgo_sb")
+        nc.sync.dma_start(wgo_sb[:], wgo)
+        idx4 = load_list(offs4, "idx4")
+        scores = []
+        for nt in range(N_TILES):
+            page = keep.tile([P, T2], F32, name=f"page1_{nt}")
+            nc.sync.dma_start(page[:], page1[P * nt : P * (nt + 1), :])
+            scores.append(page)
+
+        block_words = R_PASSES * N_BLOCK
+        early = keep.tile([P, block_words + (R_PASSES - 1) * M], U32, name="early", tag=f"slot_{SLICES - 1}",
+                          align_bytes=ALIGN)
+        last_z = keep.tile([P, M], U32, name="last_z", align_bytes=ALIGN)
+        w2_plane = keep.tile([P, N_BLOCKS * block_words], U8, name="w2_plane", align_bytes=ALIGN)
+        z_plane = keep.tile([P, R_PASSES, M], U8, name="z_plane", align_bytes=ALIGN)
+        w2_flat = w2_bf[:].rearrange("p nb b c -> p (nb b c)")
+
+        def quantise_w2(codes, first, widths):
+            done = 0
+            for width in widths:
+                nc.vector.quantize_mx(
+                    out=codes[:, done : done + width].bitcast(FP8X4),
+                    scales=w2_plane[:, first + done : first + done + width],
+                    in_=w2_flat[:, PACK * (first + done) : PACK * (first + done + width)],
+                )
+                done = done + width
+
+        quantise_w2(early, 0, (512, 256))
+        z_codes = [early[:, block_words + M * b : block_words + M * (b + 1)] for b in range(R_PASSES - 1)]
+        z_codes.append(last_z[:])
+        for b in range(R_PASSES):
+            nc.vector.quantize_mx(
+                out=z_codes[b].bitcast(FP8X4), scales=z_plane[:, b, :], in_=z_bf[b][:].rearrange("p m t -> p (m t)")
+            )
+        late = keep.tile([P, (N_BLOCKS - 1) * block_words], U32, name="late", tag=f"z_bf_{R_PASSES - 1}",
+                         align_bytes=ALIGN)
+        quantise_w2(late, block_words, (1024, 512))
+
+        for nt in range(N_TILES):
+            nb, half = divmod(nt, N_BLOCK // P)
+            codes, base = (early, 0) if nb == 0 else (late, block_words)
+            y_acc = psum.tile([P, M], F32, name="y_acc")
+            for b in range(R_PASSES):
+                c0 = block_words * nb + N_BLOCK * b + P * half
+                nc.tensor.matmul_mx(
+                    out=y_acc[:],
+                    lhsT=codes[:, c0 - base : c0 - base + P].bitcast(FP8X4),
+                    lhsT_scale=w2_plane[:, c0 : c0 + P],
+                    rhs=z_codes[b].bitcast(FP8X4),
+                    rhs_scale=z_plane[:, b, :],
+                    start=(b == 0),
+                    stop=(b == R_PASSES - 1),
+                )
+            y = ring.tile([P, M], F32, name="y")
+            nc.scalar.copy(y[:], y_acc[:])
+            nc.vector.tensor_tensor(scores[nt][:].indirect(idx4[:]), y[:], wgo_sb[:], MULT)
+            nc.sync.dma_start(out[P * nt : P * (nt + 1), :], scores[nt][:])

@@ -77,12 +77,12 @@ def tile_list_abort_page_scores_kernel(
         tab_plane = keep.tile([P, K_PASSES, T], U8, name="tab_plane", align_bytes=ALIGN)
         nc.vector.memset(tab_plane[:].bitcast(I32), 0)
         w1_plane_first = keep.tile([P, K_PASSES, PASS], U8, name="w1_plane_first", align_bytes=ALIGN)
-        nc.vector.memset(w1_plane_first[:].bitcast(I32), 0)
+        nc.gpsimd.memset(w1_plane_first[:].bitcast(I32), 0)
+        ident = keep.tile([P, P], F32, name="ident")
+        make_identity(nc, ident[:])
         w1_plane_rest = keep.tile([P, K_PASSES, H - PASS], U8, name="w1_plane_rest", align_bytes=ALIGN)
         nc.gpsimd.memset(w1_plane_rest[:].bitcast(I32), 0)
         w1_planes = [w1_plane_first] + [w1_plane_rest[:, :, PASS * b : PASS * (b + 1)] for b in range(R_PASSES - 1)]
-        ident = keep.tile([P, P], F32, name="ident")
-        make_identity(nc, ident[:])
 
         def load_tab(a):
             words = keep.tile([P, T], I32, name=f"tab_{a}")
@@ -90,12 +90,12 @@ def tile_list_abort_page_scores_kernel(
             return words
 
         wgs_rows = wgs.rearrange("(m t) j -> m t j", t=PACK)
-        wgs_first = keep.tile([P, 1, S], F32, name="wgs_first")
-        wgs_rest = keep.tile([P, PACK - 1, S], F32, name="wgs_rest")
 
-        def load_wgs(dealt, rows, quads):
-            for q in quads:
-                nc.sync.dma_start(dealt[32 * q : 32 * (q + 1)], rows)
+        def load_wgs(t0, t1):
+            dealt = keep.tile([P, t1 - t0, S], F32, name=f"wgs_{t0}")
+            for q in (0, 2, 1, 3):
+                nc.sync.dma_start(dealt[32 * q : 32 * (q + 1)], wgs_rows[:, t0:t1, :])
+            return [dealt[:, t, :] for t in range(t1 - t0)]
 
         idx = load_list(offs, "idx")
         tab = [load_tab(0)]
@@ -106,15 +106,17 @@ def tile_list_abort_page_scores_kernel(
         gain_col = load_per_row(nc.sync, gain, "gain_col")
         idx2 = load_list(offs2, "idx2")
         pages = [load_page0(0)]
-        load_wgs(wgs_first, wgs_rows[:, 0:1, :], range(QUADS))
-        idx3 = load_list(offs3, "idx3")
+        wgs_dealt = load_wgs(0, 1)
         pages.append(load_page0(1))
-        load_wgs(wgs_rest, wgs_rows[:, 1:PACK, :], range(QUADS))
-        wgs_dealt = [wgs_first[:, 0, :]] + [wgs_rest[:, t, :] for t in range(PACK - 1)]
+        wgs_dealt += load_wgs(1, 2)
+        idx3 = load_list(offs3, "idx3")
+        load_scale_rows(nc.sync, w1_plane_rest, w1_scales[:, :, PASS:H])
+        w1.append(load_w1(1))
+        pages.append(load_page0(2))
+        wgs_dealt += load_wgs(2, PACK)
         shift_col = load_per_row(nc.sync, shift, "shift_col")
         risk_col = load_per_row(nc.sync, risk, "risk_col")
-        load_scale_rows(nc.sync, w1_plane_rest, w1_scales[:, :, PASS:H])
-        w1 += [load_w1(b) for b in range(1, R_PASSES)]
+        w1.append(load_w1(2))
 
         v_scales, v_words = {}, {}
         for half in range(2):
@@ -160,8 +162,9 @@ def tile_list_abort_page_scores_kernel(
             f0 += [product(0, jt) for jt in (2 * half, 2 * half + 1)]
             parts = [square(f0[jt], f"single_{jt}", 0, 1)[0] for jt in (2 * half, 2 * half + 1)]
             turn(h[0][:, HALF * half : HALF * (half + 1)], parts, 0, 0)
+        squares = [square(f0[jt], f"square_{jt}", 1, PACK) for jt in range(J_TILES)]
         for t in range(1, PACK):
-            turn(h[t][:], [square(f0[jt], f"single_{jt}", t, t + 1)[0] for jt in range(J_TILES)], 0, t)
+            turn(h[t][:], [squares[jt][t - 1] for jt in range(J_TILES)], 0, t)
         for b in range(1, R_PASSES):
             squares = [square(product(b, jt), f"square_{jt}", 0, PACK) for jt in range(J_TILES)]
             for t in range(PACK):
@@ -179,7 +182,7 @@ def tile_list_abort_page_scores_kernel(
                 raw[:].rearrange("p t (c i) -> p c t i", i=4),
             )
 
-        z_bf = []
+        z_pairs, z_bf = [], []
 
         def recall(i):
             b, t = divmod(i, PACK)
@@ -189,14 +192,20 @@ def tile_list_abort_page_scores_kernel(
             bent = ring.tile([P, M], F32, name="bent")
             nc.scalar.activation(bent[:], x[:], ACT.Tanh, bias=shift_col[:, b, t : t + 1])
             if t == 0:
-                z_bf.append(keep.tile([P, M, PACK], BF16, name=f"z_bf_{b}", align_bytes=ALIGN))
-            nc.scalar.activation(z_bf[b][:, :, t], bent[:], ACT.Copy, scale=risk_col[:, b, t : t + 1])
+                z_pairs.append(ring.tile([P, 2, M, 2], BF16, name="z_pairs"))
+            nc.scalar.activation(z_pairs[b][:, t // 2, :, t % 2], bent[:], ACT.Copy, scale=risk_col[:, b, t : t + 1])
+            if t == PACK - 1:
+                z_bf.append(keep.tile([P, M * PACK], BF16, name=f"z_bf_{b}", align_bytes=ALIGN))
+                nc.scalar.copy(
+                    z_bf[b][:].bitcast(F32).rearrange("p (m u) -> p m u", u=2),
+                    z_pairs[b][:].rearrange("p u m e -> p u (m e)").bitcast(F32).rearrange("p u m -> p m u"),
+                )
 
         for i in range(SLICES):
-            if i >= 2:
+            if i >= 3:
                 pages.append(load_page0(i))
-                if i - 2 < N_BLOCKS * R_PASSES:
-                    round_w2(i - 2)
+            if 2 <= i < 2 + N_BLOCKS * R_PASSES:
+                round_w2(i - 2)
             width = HALF if i == 0 else S
             for j0 in range(0, S, width):
                 nc.vector.tensor_tensor(
@@ -219,7 +228,8 @@ def tile_list_abort_page_scores_kernel(
             scores.append(page)
 
         block_words = R_PASSES * N_BLOCK
-        early = keep.tile([P, block_words + (R_PASSES - 1) * M], U32, name="early", tag=f"slot_{SLICES - 1}",
+        early_words = block_words + 2 * N_BLOCK
+        early = keep.tile([P, early_words + (R_PASSES - 1) * M], U32, name="early", tag=f"slot_{SLICES - 1}",
                           align_bytes=ALIGN)
         last_z = keep.tile([P, M], U32, name="last_z", align_bytes=ALIGN)
         w2_plane = keep.tile([P, N_BLOCKS * block_words], U8, name="w2_plane", align_bytes=ALIGN)
@@ -236,23 +246,23 @@ def tile_list_abort_page_scores_kernel(
                 )
                 done = done + width
 
-        quantise_w2(early, 0, (512, 256))
-        z_codes = [early[:, block_words + M * b : block_words + M * (b + 1)] for b in range(R_PASSES - 1)]
+        quantise_w2(early, 0, (1024, 256))
+        z_codes = [early[:, early_words + M * b : early_words + M * (b + 1)] for b in range(R_PASSES - 1)]
         z_codes.append(last_z[:])
         for b in range(R_PASSES):
             nc.vector.quantize_mx(
-                out=z_codes[b].bitcast(FP8X4), scales=z_plane[:, b, :], in_=z_bf[b][:].rearrange("p m t -> p (m t)")
+                out=z_codes[b].bitcast(FP8X4), scales=z_plane[:, b, :], in_=z_bf[b][:]
             )
-        late = keep.tile([P, (N_BLOCKS - 1) * block_words], U32, name="late", tag=f"z_bf_{R_PASSES - 1}",
+        late = keep.tile([P, N_BLOCKS * block_words - early_words], U32, name="late", tag=f"z_bf_{R_PASSES - 1}",
                          align_bytes=ALIGN)
-        quantise_w2(late, block_words, (1024, 512))
+        quantise_w2(late, early_words, (1024,))
 
         for nt in range(N_TILES):
             nb, half = divmod(nt, N_BLOCK // P)
-            codes, base = (early, 0) if nb == 0 else (late, block_words)
             y_acc = psum.tile([P, M], F32, name="y_acc")
             for b in range(R_PASSES):
                 c0 = block_words * nb + N_BLOCK * b + P * half
+                codes, base = (early, 0) if c0 < early_words else (late, early_words)
                 nc.tensor.matmul_mx(
                     out=y_acc[:],
                     lhsT=codes[:, c0 - base : c0 - base + P].bitcast(FP8X4),

@@ -28,6 +28,7 @@ N_TILES = N // P
 N_BLOCK = 256
 N_BLOCKS = N // N_BLOCK
 QUADS = 4
+RUNS = ((0, 4), (4, 8), (8, 11), (11, 12))
 HALF = S // 2
 ALIGN = 64
 
@@ -77,7 +78,7 @@ def tile_list_abort_page_scores_kernel(
         tab_plane = keep.tile([P, K_PASSES, T], U8, name="tab_plane", align_bytes=ALIGN)
         nc.vector.memset(tab_plane[:].bitcast(I32), 0)
         w1_plane_first = keep.tile([P, K_PASSES, PASS], U8, name="w1_plane_first", align_bytes=ALIGN)
-        nc.gpsimd.memset(w1_plane_first[:].bitcast(I32), 0)
+        nc.vector.memset(w1_plane_first[:].bitcast(I32), 0)
         ident = keep.tile([P, P], F32, name="ident")
         make_identity(nc, ident[:])
         w1_plane_rest = keep.tile([P, K_PASSES, H - PASS], U8, name="w1_plane_rest", align_bytes=ALIGN)
@@ -146,7 +147,7 @@ def tile_list_abort_page_scores_kernel(
             return f[:].rearrange("j (p t) -> j t p", t=PACK)
 
         def square(f, name, t0, t1):
-            sq = ring.tile([P, t1 - t0, P], F32, name=name)
+            sq = ring.tile([P, t1 - t0, P], F32, name=name, bufs=1 if t1 == 1 else 2)
             nc.scalar.activation(sq[:], f[:, t0:t1, :], ACT.Square)
             return [sq[:, t, :] for t in range(t1 - t0)]
 
@@ -156,7 +157,10 @@ def tile_list_abort_page_scores_kernel(
                 nc.tensor.transpose(turned[:, P * u : P * (u + 1)], part, ident[:])
             nc.scalar.activation(h_cols, turned[:], ACT.Copy, scale=gain_col[:, b, t : t + 1])
 
-        h = [keep.tile([P, S], F32, name=f"h_{i}", tag=f"slot_{i}", align_bytes=ALIGN) for i in range(SLICES)]
+        h = []
+        for first, end in RUNS:
+            run = keep.tile([P, end - first, S], F32, name=f"h_{first}", tag=f"run_{first}", align_bytes=ALIGN)
+            h += [run[:, u, :] for u in range(end - first)]
         f0 = []
         for half in range(2):
             f0 += [product(0, jt) for jt in (2 * half, 2 * half + 1)]
@@ -164,48 +168,65 @@ def tile_list_abort_page_scores_kernel(
             turn(h[0][:, HALF * half : HALF * (half + 1)], parts, 0, 0)
         squares = [square(f0[jt], f"square_{jt}", 1, PACK) for jt in range(J_TILES)]
         for t in range(1, PACK):
-            turn(h[t][:], [squares[jt][t - 1] for jt in range(J_TILES)], 0, t)
+            turn(h[t], [squares[jt][t - 1] for jt in range(J_TILES)], 0, t)
         for b in range(1, R_PASSES):
             squares = [square(product(b, jt), f"square_{jt}", 0, PACK) for jt in range(J_TILES)]
             for t in range(PACK):
-                turn(h[PACK * b + t][:], [squares[jt][t] for jt in range(J_TILES)], b, t)
+                turn(h[PACK * b + t], [squares[jt][t] for jt in range(J_TILES)], b, t)
 
-        w2_bf = keep.tile([P, N_BLOCKS, R_PASSES, N_BLOCK * PACK], BF16, name="w2_bf", align_bytes=ALIGN)
+        block_words = R_PASSES * N_BLOCK
         w2_rows = w2.rearrange("(b p t) n -> b p t n", p=P, t=PACK)
 
-        def round_w2(piece):
-            nb, b = divmod(piece, R_PASSES)
+        def load_w2(nb, b):
             raw = ring.tile([P, PACK, N_BLOCK], F32, name="w2_raw", bufs=3)
             nc.sync.dma_start(raw[:], w2_rows[b, :, :, N_BLOCK * nb : N_BLOCK * (nb + 1)])
+            return raw
+
+        def round_w2(rounded, raw):
             nc.scalar.copy(
-                w2_bf[:, nb, b, :].rearrange("p (c i t) -> p c t i", i=4, t=PACK),
+                rounded.rearrange("p (c i t) -> p c t i", i=4, t=PACK),
                 raw[:].rearrange("p t (c i) -> p c t i", i=4),
             )
 
-        z_pairs, z_bf = [], []
+        def quantise(codes, plane, rounded):
+            nc.vector.quantize_mx(out=codes.bitcast(FP8X4), scales=plane, in_=rounded)
 
-        def recall(i):
+        def quantise_w2(codes, plane, rounded):
+            for c0, c1 in ((0, 2 * N_BLOCK), (2 * N_BLOCK, block_words)):
+                quantise(codes[:, c0:c1], plane[:, c0:c1], rounded[:, PACK * c0 : PACK * c1])
+
+        z_pairs, z_bf = {}, {}
+
+        def recall(i, x):
             b, t = divmod(i, PACK)
-            tag = f"slot_{i + 1}" if i < SLICES - 2 else f"x_{i}"
-            x = keep.tile([P, M], F32, name=f"x_{i}", tag=tag, align_bytes=ALIGN)
-            nc.vector.tensor_copy(x[:], pages[i][:].indirect(idx3[:]))
             bent = ring.tile([P, M], F32, name="bent")
-            nc.scalar.activation(bent[:], x[:], ACT.Tanh, bias=shift_col[:, b, t : t + 1])
-            if t == 0:
-                z_pairs.append(ring.tile([P, 2, M, 2], BF16, name="z_pairs"))
-            nc.scalar.activation(z_pairs[b][:, t // 2, :, t % 2], bent[:], ACT.Copy, scale=risk_col[:, b, t : t + 1])
-            if t == PACK - 1:
-                z_bf.append(keep.tile([P, M * PACK], BF16, name=f"z_bf_{b}", align_bytes=ALIGN))
-                nc.scalar.copy(
-                    z_bf[b][:].bitcast(F32).rearrange("p (m u) -> p m u", u=2),
-                    z_pairs[b][:].rearrange("p u m e -> p u (m e)").bitcast(F32).rearrange("p u m -> p m u"),
+            fetch = HALF if i == SLICES - 1 else M
+            width = HALF if b == R_PASSES - 1 else M
+            for m0 in range(0, M, width):
+                if m0 % fetch == 0:
+                    cols = slice(m0, m0 + fetch)
+                    nc.vector.tensor_copy(x[:, cols], pages[i][:].indirect(idx3[:, m0 // 16 : (m0 + fetch) // 16]))
+                    nc.scalar.activation(bent[:, cols], x[:, cols], ACT.Tanh, bias=shift_col[:, b, t : t + 1])
+                if t == 0:
+                    z_pairs[b, m0] = ring.tile([P, 2, width, 2], BF16, name=f"z_pairs_{m0}", bufs=1 if m0 else 2)
+                pairs = z_pairs[b, m0]
+                nc.scalar.activation(
+                    pairs[:, t // 2, :, t % 2], bent[:, m0 : m0 + width], ACT.Copy, scale=risk_col[:, b, t : t + 1]
                 )
+                if t == PACK - 1:
+                    z_bf[b, m0] = keep.tile([P, width * PACK], BF16, name=f"z_bf_{b}_{m0}", align_bytes=ALIGN)
+                    nc.scalar.copy(
+                        z_bf[b, m0][:].bitcast(F32).rearrange("p (m u) -> p m u", u=2),
+                        pairs[:].rearrange("p u m e -> p u (m e)").bitcast(F32).rearrange("p u m -> p m u"),
+                    )
 
+        w2_bf = [keep.tile([P, block_words * PACK], BF16, name=f"w2_bf_{nb}", align_bytes=ALIGN) for nb in range(N_BLOCKS)]
         for i in range(SLICES):
             if i >= 3:
                 pages.append(load_page0(i))
             if 2 <= i < 2 + N_BLOCKS * R_PASSES:
-                round_w2(i - 2)
+                nb, b = divmod(i - 2, R_PASSES)
+                round_w2(w2_bf[nb][:, PACK * N_BLOCK * b : PACK * N_BLOCK * (b + 1)], load_w2(nb, b))
             width = HALF if i == 0 else S
             for j0 in range(0, S, width):
                 nc.vector.tensor_tensor(
@@ -214,9 +235,12 @@ def tile_list_abort_page_scores_kernel(
                     wgs_dealt[i % PACK][:, j0 : j0 + width],
                     MULT,
                 )
-            if i >= 1:
-                recall(i - 1)
-        recall(SLICES - 1)
+            for first, end in RUNS:
+                if i == end - 1:
+                    tag = f"run_{first}" if end < SLICES else "x_last"
+                    x = keep.tile([P, end - first, M], F32, name=f"x_{first}", tag=tag, align_bytes=ALIGN)
+                    for u in range(end - first):
+                        recall(first + u, x[:, u, :])
 
         wgo_sb = keep.tile([P, M], F32, name="wgo_sb")
         nc.sync.dma_start(wgo_sb[:], wgo)
@@ -227,52 +251,45 @@ def tile_list_abort_page_scores_kernel(
             nc.sync.dma_start(page[:], page1[P * nt : P * (nt + 1), :])
             scores.append(page)
 
-        block_words = R_PASSES * N_BLOCK
-        early_words = block_words + 2 * N_BLOCK
-        early = keep.tile([P, early_words + (R_PASSES - 1) * M], U32, name="early", tag=f"slot_{SLICES - 1}",
-                          align_bytes=ALIGN)
+        last = R_PASSES - 1
+        early = keep.tile([P, N_BLOCKS * block_words + last * M], U32, name="early", tag=f"run_{SLICES - 1}", align_bytes=ALIGN)
         last_z = keep.tile([P, M], U32, name="last_z", align_bytes=ALIGN)
-        w2_plane = keep.tile([P, N_BLOCKS * block_words], U8, name="w2_plane", align_bytes=ALIGN)
+        w2_plane = keep.tile([P, N_BLOCKS, block_words], U8, name="w2_plane", align_bytes=ALIGN)
         z_plane = keep.tile([P, R_PASSES, M], U8, name="z_plane", align_bytes=ALIGN)
-        w2_flat = w2_bf[:].rearrange("p nb b c -> p (nb b c)")
+        w2_codes = [early[:, block_words * nb : block_words * (nb + 1)] for nb in range(N_BLOCKS)]
+        z_first = N_BLOCKS * block_words
+        z_codes = [early[:, z_first + M * b : z_first + M * (b + 1)] for b in range(last)] + [last_z[:]]
+        quantise_w2(w2_codes[0], w2_plane[:, 0, :], w2_bf[0])
+        for b in range(last):
+            quantise(z_codes[b], z_plane[:, b, :], z_bf[b, 0][:])
+        quantise(last_z[:, 0:HALF], z_plane[:, last, 0:HALF], z_bf[last, 0][:])
+        quantise(last_z[:, HALF:M], z_plane[:, last, HALF:M], z_bf[last, HALF][:])
+        for nb in range(1, N_BLOCKS):
+            quantise_w2(w2_codes[nb], w2_plane[:, nb, :], w2_bf[nb])
 
-        def quantise_w2(codes, first, widths):
-            done = 0
-            for width in widths:
-                nc.vector.quantize_mx(
-                    out=codes[:, done : done + width].bitcast(FP8X4),
-                    scales=w2_plane[:, first + done : first + done + width],
-                    in_=w2_flat[:, PACK * (first + done) : PACK * (first + done + width)],
-                )
-                done = done + width
-
-        quantise_w2(early, 0, (1024, 256))
-        z_codes = [early[:, early_words + M * b : early_words + M * (b + 1)] for b in range(R_PASSES - 1)]
-        z_codes.append(last_z[:])
-        for b in range(R_PASSES):
-            nc.vector.quantize_mx(
-                out=z_codes[b].bitcast(FP8X4), scales=z_plane[:, b, :], in_=z_bf[b][:]
-            )
-        late = keep.tile([P, N_BLOCKS * block_words - early_words], U32, name="late", tag=f"z_bf_{R_PASSES - 1}",
-                         align_bytes=ALIGN)
-        quantise_w2(late, early_words, (1024,))
-
-        for nt in range(N_TILES):
+        def score(nt, m0, m1):
             nb, half = divmod(nt, N_BLOCK // P)
-            y_acc = psum.tile([P, M], F32, name="y_acc")
+            y_acc = psum.tile([P, m1 - m0], F32, name="y_acc")
             for b in range(R_PASSES):
-                c0 = block_words * nb + N_BLOCK * b + P * half
-                codes, base = (early, 0) if c0 < early_words else (late, early_words)
+                cols = slice(N_BLOCK * b + P * half, N_BLOCK * b + P * (half + 1))
                 nc.tensor.matmul_mx(
                     out=y_acc[:],
-                    lhsT=codes[:, c0 - base : c0 - base + P].bitcast(FP8X4),
-                    lhsT_scale=w2_plane[:, c0 : c0 + P],
-                    rhs=z_codes[b].bitcast(FP8X4),
-                    rhs_scale=z_plane[:, b, :],
+                    lhsT=w2_codes[nb][:, cols].bitcast(FP8X4),
+                    lhsT_scale=w2_plane[:, nb, cols],
+                    rhs=z_codes[b][:, m0:m1].bitcast(FP8X4),
+                    rhs_scale=z_plane[:, b, m0:m1],
                     start=(b == 0),
-                    stop=(b == R_PASSES - 1),
+                    stop=(b == last),
                 )
-            y = ring.tile([P, M], F32, name="y")
+            y = ring.tile([P, m1 - m0], F32, name="y")
             nc.scalar.copy(y[:], y_acc[:])
-            nc.vector.tensor_tensor(scores[nt][:].indirect(idx4[:]), y[:], wgo_sb[:], MULT)
-            nc.sync.dma_start(out[P * nt : P * (nt + 1), :], scores[nt][:])
+            nc.vector.tensor_tensor(
+                scores[nt][:].indirect(idx4[:, m0 // 16 : m1 // 16]), y[:], wgo_sb[:, m0:m1], MULT
+            )
+            if m1 == M:
+                nc.sync.dma_start(out[P * nt : P * (nt + 1), :], scores[nt][:])
+
+        score(0, 0, HALF)
+        score(0, HALF, M)
+        for nt in range(1, N_TILES):
+            score(nt, 0, M)

from contextlib import ExitStack

import concourse.mybir as mybir
from concourse.masks import make_identity

K, H, N, T, S, M, T2 = 1024, 1536, 768, 2048, 512, 512, 1024
FLOPS = 2 * K * H * S + 2 * H * N * M

F32 = mybir.dt.float32
BF16 = mybir.dt.bfloat16
I32 = mybir.dt.int32
U32 = mybir.dt.uint32
U16 = mybir.dt.uint16
U8 = mybir.dt.uint8
FP8X4 = mybir.dt.float8_e4m3fn_x4
FP4X4 = mybir.dt.float4_e2m1fn_x4
ACT = mybir.ActivationFunctionType
MULT = mybir.AluOpType.mult

P = 128
PACK = 4
PASS = P * PACK
K_PASSES = K // PASS
R_PASSES = H // PASS
SLICES = R_PASSES * PACK
J_TILES = S // P
N_TILES = N // P
N_BLOCK = 256
N_BLOCKS = N // N_BLOCK
QUADS = 4
RUNS = ((0, 4), (4, 8), (8, 11), (11, 12))
HALF = S // 2
ALIGN = 64


def tile_list_abort_page_scores_kernel(
    tc, tab_words, tab_scales, w1_words, w1_scales, gain, wgs, page0, shift, risk, w2, wgo, page1,
    offs, offs2, offs3, offs4, out,
):
    nc = tc.nc
    with ExitStack() as ctx:
        keep = ctx.enter_context(tc.tile_pool(name="keep", bufs=1))
        ring = ctx.enter_context(tc.tile_pool(name="ring", bufs=2))
        psum = ctx.enter_context(tc.psum_pool(name="psum", bufs=2))

        def load_list(src, name):
            lst = keep.tile([P, S // 16], U16, name=name)
            nc.sync.dma_start(lst[:], src)
            return lst

        def load_per_row(queue, vec, name):
            col = keep.tile([P, R_PASSES, PACK], F32, name=name)
            queue.dma_start(col[:], vec.rearrange("(b p t) -> p b t", p=P, t=PACK))
            return col

        def load_scale_rows(queue, plane, scales):
            for q in range(QUADS):
                queue.dma_start(
                    plane[32 * q : 32 * q + 4, :, :].bitcast(I32),
                    scales[:, 4 * q : 4 * q + 4, :].rearrange("a r c -> r a c").bitcast(I32),
                )

        page0_rows = page0.rearrange("(b p t) c -> b t p c", p=P, t=PACK)

        def load_page0(i):
            page = keep.tile([P, T2], F32, name=f"page0_{i}")
            nc.sync.dma_start(page[:], page0_rows[i // PACK, i % PACK])
            return page

        def load_w1(b):
            words = keep.tile([P, K_PASSES, 2 * PASS], U8, name=f"w1_words_{b}", align_bytes=ALIGN)
            nc.sync.dma_start(
                words[:].bitcast(I32),
                w1_words[:, :, 2 * PASS * b : 2 * PASS * (b + 1)].rearrange("a p c -> p a c").bitcast(I32),
            )
            return words

        tab_plane = keep.tile([P, K_PASSES, T], U8, name="tab_plane", align_bytes=ALIGN)
        nc.vector.memset(tab_plane[:].bitcast(I32), 0)
        w1_plane_first = keep.tile([P, K_PASSES, PASS], U8, name="w1_plane_first", align_bytes=ALIGN)
        nc.vector.memset(w1_plane_first[:].bitcast(I32), 0)
        ident = keep.tile([P, P], F32, name="ident")
        make_identity(nc, ident[:])
        w1_plane_rest = keep.tile([P, K_PASSES, H - PASS], U8, name="w1_plane_rest", align_bytes=ALIGN)
        nc.gpsimd.memset(w1_plane_rest[:].bitcast(I32), 0)
        w1_planes = [w1_plane_first] + [w1_plane_rest[:, :, PASS * b : PASS * (b + 1)] for b in range(R_PASSES - 1)]

        def load_tab(a):
            words = keep.tile([P, T], I32, name=f"tab_{a}")
            nc.sync.dma_start(words[:], tab_words[a].rearrange("p t i -> p (t i)").bitcast(I32))
            return words

        wgs_rows = wgs.rearrange("(m t) j -> m t j", t=PACK)

        def load_wgs(t0, t1):
            dealt = keep.tile([P, t1 - t0, S], F32, name=f"wgs_{t0}")
            for q in (0, 2, 1, 3):
                nc.sync.dma_start(dealt[32 * q : 32 * (q + 1)], wgs_rows[:, t0:t1, :])
            return [dealt[:, t, :] for t in range(t1 - t0)]

        idx = load_list(offs, "idx")
        tab = [load_tab(0)]
        load_scale_rows(nc.sync, tab_plane, tab_scales)
        w1 = [load_w1(0)]
        load_scale_rows(nc.sync, w1_plane_first, w1_scales[:, :, 0:PASS])
        tab.append(load_tab(1))
        gain_col = load_per_row(nc.sync, gain, "gain_col")
        idx2 = load_list(offs2, "idx2")
        pages = [load_page0(0)]
        wgs_dealt = load_wgs(0, 1)
        pages.append(load_page0(1))
        wgs_dealt += load_wgs(1, 2)
        idx3 = load_list(offs3, "idx3")
        load_scale_rows(nc.sync, w1_plane_rest, w1_scales[:, :, PASS:H])
        w1.append(load_w1(1))
        pages.append(load_page0(2))
        wgs_dealt += load_wgs(2, PACK)
        shift_col = load_per_row(nc.sync, shift, "shift_col")
        risk_col = load_per_row(nc.sync, risk, "risk_col")
        w1.append(load_w1(2))

        v_scales, v_words = {}, {}
        for half in range(2):
            entries = idx[:, HALF // 16 * half : HALF // 16 * (half + 1)]
            for a in range(K_PASSES):
                picked = keep.tile([P, HALF], U8, name=f"v_scales_{a}_{half}", align_bytes=ALIGN)
                nc.vector.tensor_copy(picked[:], tab_plane[:, a, :].indirect(entries))
                v_scales[a, half] = picked
            for a in range(K_PASSES):
                picked = keep.tile([P, HALF], U32, name=f"v_words_{a}_{half}", align_bytes=ALIGN)
                nc.vector.tensor_copy(picked[:], tab[a][:].bitcast(U32).indirect(entries))
                v_words[a, half] = picked

        def product(b, jt):
            half, cols = jt // 2, slice(P * (jt % 2), P * (jt % 2 + 1))
            f = psum.tile([P, PASS], F32, name="f", bufs=4)
            for a in range(K_PASSES):
                nc.tensor.matmul_mx(
                    out=f[:],
                    lhsT=v_words[a, half][:, cols].bitcast(FP8X4),
                    lhsT_scale=v_scales[a, half][:, cols],
                    rhs=w1[b][:, a, :].bitcast(FP4X4),
                    rhs_scale=w1_planes[b][:, a, :],
                    start=(a == 0),
                    stop=(a == K_PASSES - 1),
                )
            return f[:].rearrange("j (p t) -> j t p", t=PACK)

        def square(f, name, t0, t1):
            sq = ring.tile([P, t1 - t0, P], F32, name=name, bufs=1 if t1 == 1 else 2)
            nc.scalar.activation(sq[:], f[:, t0:t1, :], ACT.Square)
            return [sq[:, t, :] for t in range(t1 - t0)]

        def turn(h_cols, parts, b, t):
            turned = psum.tile([P, P * len(parts)], F32, name="turned")
            for u, part in enumerate(parts):
                nc.tensor.transpose(turned[:, P * u : P * (u + 1)], part, ident[:])
            nc.scalar.activation(h_cols, turned[:], ACT.Copy, scale=gain_col[:, b, t : t + 1])

        h = []
        for first, end in RUNS:
            run = keep.tile([P, end - first, S], F32, name=f"h_{first}", tag=f"run_{first}", align_bytes=ALIGN)
            h += [run[:, u, :] for u in range(end - first)]
        f0 = []
        for half in range(2):
            f0 += [product(0, jt) for jt in (2 * half, 2 * half + 1)]
            parts = [square(f0[jt], f"single_{jt}", 0, 1)[0] for jt in (2 * half, 2 * half + 1)]
            turn(h[0][:, HALF * half : HALF * (half + 1)], parts, 0, 0)
        squares = [square(f0[jt], f"square_{jt}", 1, PACK) for jt in range(J_TILES)]
        for t in range(1, PACK):
            turn(h[t], [squares[jt][t - 1] for jt in range(J_TILES)], 0, t)
        for b in range(1, R_PASSES):
            squares = [square(product(b, jt), f"square_{jt}", 0, PACK) for jt in range(J_TILES)]
            for t in range(PACK):
                turn(h[PACK * b + t], [squares[jt][t] for jt in range(J_TILES)], b, t)

        block_words = R_PASSES * N_BLOCK
        w2_rows = w2.rearrange("(b p t) n -> b p t n", p=P, t=PACK)

        def load_w2(nb, b):
            raw = ring.tile([P, PACK, N_BLOCK], F32, name="w2_raw", bufs=3)
            nc.sync.dma_start(raw[:], w2_rows[b, :, :, N_BLOCK * nb : N_BLOCK * (nb + 1)])
            return raw

        def round_w2(rounded, raw):
            nc.scalar.copy(
                rounded.rearrange("p (c i t) -> p c t i", i=4, t=PACK),
                raw[:].rearrange("p t (c i) -> p c t i", i=4),
            )

        def quantise(codes, plane, rounded):
            nc.vector.quantize_mx(out=codes.bitcast(FP8X4), scales=plane, in_=rounded)

        def quantise_w2(codes, plane, rounded):
            for c0, c1 in ((0, 2 * N_BLOCK), (2 * N_BLOCK, block_words)):
                quantise(codes[:, c0:c1], plane[:, c0:c1], rounded[:, PACK * c0 : PACK * c1])

        z_pairs, z_bf = {}, {}

        def recall(i, x):
            b, t = divmod(i, PACK)
            bent = ring.tile([P, M], F32, name="bent")
            fetch = HALF if i == SLICES - 1 else M
            width = HALF if b == R_PASSES - 1 else M
            for m0 in range(0, M, width):
                if m0 % fetch == 0:
                    cols = slice(m0, m0 + fetch)
                    nc.vector.tensor_copy(x[:, cols], pages[i][:].indirect(idx3[:, m0 // 16 : (m0 + fetch) // 16]))
                    nc.scalar.activation(bent[:, cols], x[:, cols], ACT.Tanh, bias=shift_col[:, b, t : t + 1])
                if t == 0:
                    z_pairs[b, m0] = ring.tile([P, 2, width, 2], BF16, name=f"z_pairs_{m0}", bufs=1 if m0 else 2)
                pairs = z_pairs[b, m0]
                nc.scalar.activation(
                    pairs[:, t // 2, :, t % 2], bent[:, m0 : m0 + width], ACT.Copy, scale=risk_col[:, b, t : t + 1]
                )
                if t == PACK - 1:
                    z_bf[b, m0] = keep.tile([P, width * PACK], BF16, name=f"z_bf_{b}_{m0}", align_bytes=ALIGN)
                    nc.scalar.copy(
                        z_bf[b, m0][:].bitcast(F32).rearrange("p (m u) -> p m u", u=2),
                        pairs[:].rearrange("p u m e -> p u (m e)").bitcast(F32).rearrange("p u m -> p m u"),
                    )

        w2_bf = [keep.tile([P, block_words * PACK], BF16, name=f"w2_bf_{nb}", align_bytes=ALIGN) for nb in range(N_BLOCKS)]
        for i in range(SLICES):
            if i >= 3:
                pages.append(load_page0(i))
            if 2 <= i < 2 + N_BLOCKS * R_PASSES:
                nb, b = divmod(i - 2, R_PASSES)
                round_w2(w2_bf[nb][:, PACK * N_BLOCK * b : PACK * N_BLOCK * (b + 1)], load_w2(nb, b))
            width = HALF if i == 0 else S
            for j0 in range(0, S, width):
                nc.vector.tensor_tensor(
                    pages[i][:].indirect(idx2[:, j0 // 16 : (j0 + width) // 16]),
                    h[i][:, j0 : j0 + width],
                    wgs_dealt[i % PACK][:, j0 : j0 + width],
                    MULT,
                )
            for first, end in RUNS:
                if i == end - 1:
                    tag = f"run_{first}" if end < SLICES else "x_last"
                    x = keep.tile([P, end - first, M], F32, name=f"x_{first}", tag=tag, align_bytes=ALIGN)
                    for u in range(end - first):
                        recall(first + u, x[:, u, :])

        wgo_sb = keep.tile([P, M], F32, name="wgo_sb")
        nc.sync.dma_start(wgo_sb[:], wgo)
        idx4 = load_list(offs4, "idx4")
        scores = []
        for nt in range(N_TILES):
            page = keep.tile([P, T2], F32, name=f"page1_{nt}")
            nc.sync.dma_start(page[:], page1[P * nt : P * (nt + 1), :])
            scores.append(page)

        last = R_PASSES - 1
        early = keep.tile([P, N_BLOCKS * block_words + last * M], U32, name="early", tag=f"run_{SLICES - 1}", align_bytes=ALIGN)
        last_z = keep.tile([P, M], U32, name="last_z", align_bytes=ALIGN)
        w2_plane = keep.tile([P, N_BLOCKS, block_words], U8, name="w2_plane", align_bytes=ALIGN)
        z_plane = keep.tile([P, R_PASSES, M], U8, name="z_plane", align_bytes=ALIGN)
        w2_codes = [early[:, block_words * nb : block_words * (nb + 1)] for nb in range(N_BLOCKS)]
        z_first = N_BLOCKS * block_words
        z_codes = [early[:, z_first + M * b : z_first + M * (b + 1)] for b in range(last)] + [last_z[:]]
        quantise_w2(w2_codes[0], w2_plane[:, 0, :], w2_bf[0])
        for b in range(last):
            quantise(z_codes[b], z_plane[:, b, :], z_bf[b, 0][:])
        quantise(last_z[:, 0:HALF], z_plane[:, last, 0:HALF], z_bf[last, 0][:])
        quantise(last_z[:, HALF:M], z_plane[:, last, HALF:M], z_bf[last, HALF][:])
        for nb in range(1, N_BLOCKS):
            quantise_w2(w2_codes[nb], w2_plane[:, nb, :], w2_bf[nb])

        def score(nt, m0, m1):
            nb, half = divmod(nt, N_BLOCK // P)
            y_acc = psum.tile([P, m1 - m0], F32, name="y_acc")
            for b in range(R_PASSES):
                cols = slice(N_BLOCK * b + P * half, N_BLOCK * b + P * (half + 1))
                nc.tensor.matmul_mx(
                    out=y_acc[:],
                    lhsT=w2_codes[nb][:, cols].bitcast(FP8X4),
                    lhsT_scale=w2_plane[:, nb, cols],
                    rhs=z_codes[b][:, m0:m1].bitcast(FP8X4),
                    rhs_scale=z_plane[:, b, m0:m1],
                    start=(b == 0),
                    stop=(b == last),
                )
            y = ring.tile([P, m1 - m0], F32, name="y")
            nc.scalar.copy(y[:], y_acc[:])
            nc.vector.tensor_tensor(
                scores[nt][:].indirect(idx4[:, m0 // 16 : m1 // 16]), y[:], wgo_sb[:, m0:m1], MULT
            )
            if m1 == M:
                nc.sync.dma_start(out[P * nt : P * (nt + 1), :], scores[nt][:])

        score(0, 0, HALF)
        score(0, HALF, M)
        for nt in range(1, N_TILES):
            score(nt, 0, M)
